import numpy as np
import ml_dtypes


def mxq(x, axis, fmt="e4m3"):
    dtype, down = {"e4m3": (ml_dtypes.float8_e4m3fn, 7), "e5m2": (ml_dtypes.float8_e5m2, 14)}[fmt]
    v = np.moveaxis(np.asarray(x, np.float32).astype(ml_dtypes.bfloat16).astype(np.float64), axis, -1)
    blocks = v.reshape(v.shape[:-1] + (-1, 32))
    amax = np.abs(blocks).max(-1, keepdims=True)
    byte = np.maximum(np.where(amax > 0, np.frexp(amax)[1] - 1 + 127, 0) - down, 1)
    scale = np.exp2(byte - 127.0)
    codes = (blocks / scale).astype(np.float32).astype(dtype).astype(np.float64)
    return np.moveaxis((codes * scale).reshape(v.shape), -1, axis)


WIDE = False


def mx_kscale(k):
    if not WIDE:
        return np.ones(k)
    levels = np.array([10, -10, 5, -5, 0])
    if k % 512:
        return np.exp2(np.random.permutation(np.resize(levels, k // 32))).repeat(32)
    a = np.empty((k // 512, 16))
    for p in range(k // 512):
        a[p, :8] = np.random.permutation(np.resize(levels, 8))
        for g in range(8):
            far = levels[np.abs(levels - a[p, g]) >= 10]
            a[p, g + 8] = far[np.random.randint(len(far))]
    return np.exp2(a.ravel()).repeat(32)


def f64(x):
    return np.asarray(x).astype(np.float64)


def striped(idx):
    return np.tile(idx.reshape(-1, 16).T, (8, 1)).astype(np.uint16)


def unstriped(offs):
    return offs[:16].T.reshape(-1).astype(np.int64)


def striped8(idx):
    return np.concatenate([x.reshape(-1, 16).T for x in idx]).astype(np.uint16)


def runs(offs, k):
    lists = np.stack([offs[16 * r : 16 * r + 16].T.reshape(-1) for r in range(8)]).astype(np.int64)
    return lists[np.arange(k) % 512 // 64]


def pack_weight(w):
    k, n = w.shape
    w = f64(np.asarray(w, np.float32).astype(ml_dtypes.bfloat16)).reshape(k // 32, 32, n)
    amax = np.abs(w).max(1)
    byte = np.clip(np.where(amax > 0, np.frexp(amax)[1] - 1 + 127 - 7, 1), 1, 254)
    scaled = (w * np.exp2(127.0 - byte)[:, None, :]).reshape(k, n).astype(np.float32)
    words = np.ascontiguousarray(scaled.reshape(k // 512, 128, 4, n).transpose(0, 1, 3, 2)).astype(ml_dtypes.float8_e4m3fn).view(np.uint8)
    return words, np.ascontiguousarray(byte.astype(np.uint8).reshape(k // 512, 16, n))


def unpack_weight(words, scales):
    g, p, n, _ = words.shape
    vals = np.ascontiguousarray(words).view(ml_dtypes.float8_e4m3fn).astype(np.float64) * np.repeat(np.exp2(scales.astype(np.float64) - 127.0), 8, axis=1)[..., None]
    return vals.transpose(0, 1, 3, 2).reshape(g * 512, n)


K, T, S, N, H, W = 512, 2048, 512, 512, 512, 2048


def setup_inputs():
    n = np.random.standard_normal
    s = mx_kscale(K)[:, None]
    u = mx_kscale(H)
    packed_xT = pack_weight(n((K, T)) * s)
    return {
        "x_words": packed_xT[0],
        "x_scales": packed_xT[1],
        "w1": (n((K, H)) / np.sqrt(K) / s).astype(np.float32),
        "gn": (np.random.uniform(0.5, 1.5, (H, 1)) * u[:, None]).astype(np.float32),
        "w2": (n((H, N)) / np.sqrt(2 * H) / u[:, None]).astype(np.float32),
        "w3": (n((K, N)) / np.sqrt(2 * K) / s).astype(np.float32),
        "offs": striped(np.random.permutation(T)[:S]),
        "n1": striped8(np.stack([np.random.permutation(S) for _ in range(8)])),
        "n2": striped8(np.stack([np.random.permutation(S) for _ in range(8)])),
        "hz": striped8(np.random.randint(0, T, (8, S))),
        "n3": striped(np.random.randint(0, S, W)),
    }


def reference(x_words, x_scales, w1, gn, w2, w3, offs, n1, n2, hz, n3):
    xq = unpack_weight(x_words, x_scales)[:, unstriped(offs)]
    y = mxq(f64(w1), 0, "e4m3").T @ xq
    z = f64(gn) * ((y[np.arange(H)[:, None], runs(n1, H)]) * (y[np.arange(H)[:, None], runs(n2, H)]))
    x_hz = unpack_weight(x_words, x_scales)[np.arange(K)[:, None], runs(hz, K)]
    h = mxq(f64(w2), 0, "e4m3").T @ mxq(z, 0, "e4m3") + mxq(f64(w3), 0, "e4m3").T @ x_hz
    mb = h[:, unstriped(n3)]
    mx = mb.reshape(N, S, 4).max(axis=2)
    mn = mb.reshape(N, S, 4).min(axis=2)
    return mx - (0.5 * mn)

@@ -1,0 +1,231 @@
+from contextlib import ExitStack
+
+import concourse.mybir as mybir
+
+K, T, S, N, H, W = 512, 2048, 512, 512, 512, 2048
+FLOPS = 3 * 2 * 512 * 512 * 512
+
+F32 = mybir.dt.float32
+BF16 = mybir.dt.bfloat16
+I32 = mybir.dt.int32
+U32 = mybir.dt.uint32
+U16 = mybir.dt.uint16
+U8 = mybir.dt.uint8
+FP8X4 = mybir.dt.float8_e4m3fn_x4
+COPY = mybir.ActivationFunctionType.Copy
+MULT = mybir.AluOpType.mult
+ADD = mybir.AluOpType.add
+MAX = mybir.AluOpType.max
+MIN = mybir.AluOpType.min
+
+P = 128
+PACK = 4
+PER_COLUMN = 16
+HALF = 256
+MEMBERS = 4
+SPARE = 32
+GATHER = 512
+BOTH_ON_SCALAR = 3
+
+
+def entries(list_tile, first, count):
+    return list_tile[:, first // PER_COLUMN : (first + count) // PER_COLUMN]
+
+
+def tile_picked_mixhprodgspan_none_p_kernel(
+    tc, x_words, x_scales, w1, gn, w2, w3, offs, n1, n2, hz, n3, out
+):
+    nc = tc.nc
+    with ExitStack() as ctx:
+        lists = ctx.enter_context(tc.tile_pool(name="lists", bufs=1))
+        keep = ctx.enter_context(tc.tile_pool(name="keep", bufs=1))
+        psum = ctx.enter_context(tc.psum_pool(name="psum", bufs=1))
+
+        def load_list(name, source):
+            list_tile = lists.tile([P, source.shape[1]], U16, name=name)
+            nc.sync.dma_start(list_tile[:], source)
+            return list_tile
+
+        def load_weight_half(name, w, half):
+            raw = keep.tile([P, PACK, HALF], F32, name=name)
+            cols = slice(half * HALF, (half + 1) * HALF)
+            nc.sync.dma_start(raw[:], w.rearrange("(p j) c -> p j c", j=PACK)[:, :, cols])
+            return raw
+
+        def interleave(name, planes, copy=nc.vector.tensor_copy):
+            grouped = keep.tile([P, HALF, PACK], BF16, name=name, align_bytes=64)
+            copy(
+                grouped[:].rearrange("p (c i) j -> p c j i", i=4),
+                planes[:].rearrange("p j (c i) -> p c j i", i=4),
+            )
+            return grouped
+
+        def quantize(name, flat, width):
+            codes = keep.tile([P, width], U32, name=name + "_codes", align_bytes=64)
+            scales = keep.tile([P, width], U8, name=name + "_scales", align_bytes=64)
+            nc.vector.quantize_mx(codes[:].bitcast(FP8X4), scales[:], flat)
+            return codes, scales
+
+        def quantize_half(name, grouped):
+            return quantize(name, grouped[:].rearrange("p c j -> p (c j)"), HALF)
+
+        byte_table = keep.tile([P, T], U8, name="byte_table", align_bytes=64)
+        nc.gpsimd.memset(byte_table[:].bitcast(I32), 0)
+        scale_rows = x_scales[0]
+        for u in range(4):
+            partition_step, row_step = (16, 2) if u < 2 else (32, 4)
+            nc.sync.dma_start(
+                byte_table[u:P:partition_step, :].bitcast(I32),
+                scale_rows[u:16:row_step, :].bitcast(I32),
+            )
+        offs_t = load_list("offs_t", offs)
+        hz_t = load_list("hz_t", hz)
+        word_table = keep.tile([P, T], I32, name="word_table", align_bytes=64)
+        nc.sync.dma_start(word_table[:], x_words[0].rearrange("p n t -> p (n t)").bitcast(I32))
+        w1_raw = [load_weight_half("w1_raw%d" % h, w1, h) for h in range(2)]
+        n1_t = load_list("n1_t", n1)
+        n2_t = load_list("n2_t", n2)
+        gain = keep.tile([P, PACK], F32, name="gain")
+        nc.sync.dma_start(gain[:], gn.rearrange("(p t) o -> p (t o)", t=PACK))
+        w3_raw = [load_weight_half("w3_raw0", w3, 0)]
+        w2_raw = [load_weight_half("w2_raw0", w2, 0)]
+        n3_t = load_list("n3_t", n3)
+        w3_raw.append(load_weight_half("w3_raw1", w3, 1))
+        w2_raw.append(load_weight_half("w2_raw1", w2, 1))
+
+        h_rows = [keep.tile([P, S + SPARE], F32, name="h_rows%d" % m) for m in range(4)]
+        for m in range(4):
+            nc.gpsimd.memset(h_rows[m][:, S:], 0.0)
+
+        def gather_packed(name, table, dtype, list_tile):
+            picked = keep.tile([P, S], dtype, name=name, align_bytes=64)
+            nc.vector.tensor_copy(picked[:], table.indirect(list_tile[:]))
+            return picked
+
+        words = word_table[:].bitcast(U32)
+        x_bytes = gather_packed("x_bytes", byte_table[:], U8, offs_t)
+        hz_bytes_raw = gather_packed("hz_bytes_raw", byte_table[:], U8, hz_t)
+        x_codes = gather_packed("x_codes", words, U32, offs_t)
+
+        hz_bytes = keep.tile([P, S], U8, name="hz_bytes", align_bytes=64)
+        nc.vector.tensor_copy(hz_bytes[:].bitcast(I32), hz_bytes_raw[:].bitcast(I32))
+
+        w1_grouped = keep.tile([P, PACK, P, PACK], BF16, name="w1_grouped", align_bytes=64)
+        for half in range(2):
+            dst = w1_grouped[:, :, half * 64 : (half + 1) * 64, :].rearrange("p t m j -> p m t j")
+            src = w1_raw[half][:].rearrange("p j (m t) -> p m t j", t=PACK)
+            if half == 0:
+                nc.scalar.copy(dst, src)
+            else:
+                nc.vector.tensor_copy(dst, src)
+        w1_q = [
+            quantize("w1_%d" % t, w1_grouped[:, t, :, :].rearrange("p m j -> p (m j)"), P)
+            for t in range(PACK)
+        ]
+        hz_codes = gather_packed("hz_codes", words, U32, hz_t)
+        for u in range(2):
+            nc.sync.dma_start(
+                hz_bytes[2 + u : P : 32, :].bitcast(I32), hz_bytes_raw[16 + u : P : 32, :].bitcast(I32)
+            )
+
+        y_rows = []
+        for t in range(PACK):
+            bank = psum.tile([P, S], F32, name="y_bank%d" % t)
+            codes, scales = w1_q[t]
+            nc.tensor.matmul_mx(
+                bank[:], lhsT=codes[:].bitcast(FP8X4), lhsT_scale=scales[:],
+                rhs=x_codes[:].bitcast(FP8X4), rhs_scale=x_bytes[:], start=True, stop=True,
+            )
+            rows = keep.tile([P, S], F32, name="y_rows%d" % t)
+            nc.scalar.copy(rows[:], bank[:])
+            y_rows.append(rows)
+
+        w3_q = [quantize_half("w3_0", interleave("w3_grouped0", w3_raw[0]))]
+
+        gained = {}
+        for t in range(PACK):
+            if t != BOTH_ON_SCALAR:
+                gained[t] = keep.tile([P, S], F32, name="gained%d" % t)
+                nc.vector.tensor_scalar(gained[t][:], y_rows[t][:], gain[:, t : t + 1], None, MULT)
+
+        def z_planes(half):
+            planes = keep.tile([P, PACK, HALF], F32, name="z_planes%d" % half)
+            by_n1 = entries(n1_t, half * HALF, HALF)
+            by_n2 = entries(n2_t, half * HALF, HALF)
+            for t in range(PACK):
+                first = keep.tile([P, HALF], F32, name="first%d_%d" % (half, t))
+                nc.scalar.activation(first[:], y_rows[t][:].indirect(by_n1), COPY)
+                if t == BOTH_ON_SCALAR:
+                    second = keep.tile([P, HALF], F32, name="second%d" % half)
+                    nc.scalar.activation(second[:], y_rows[t][:].indirect(by_n2), COPY)
+                    nc.vector.scalar_tensor_tensor(
+                        planes[:, t, :], first[:], gain[:, t : t + 1], second[:], MULT, MULT
+                    )
+                else:
+                    nc.vector.tensor_tensor(planes[:, t, :], gained[t][:].indirect(by_n2), first[:], MULT)
+            return planes
+
+        z_grouped0 = interleave("z_grouped0", z_planes(0))
+        w2_grouped0 = interleave("w2_grouped0", w2_raw[0])
+        z_q = [quantize_half("z_0", z_grouped0)]
+        w2_q = [quantize_half("w2_0", w2_grouped0)]
+        z_q.append(quantize_half("z_1", interleave("z_grouped1", z_planes(1))))
+
+        def h_products(m):
+            bank = psum.tile([P, S], F32, name="h_bank%d" % m)
+            m_cols = slice((m % 2) * P, (m % 2 + 1) * P)
+            for half in range(2):
+                cols = slice(half * HALF, (half + 1) * HALF)
+                nc.tensor.matmul_mx(
+                    bank[:, cols], lhsT=w3_q[m // 2][0][:, m_cols].bitcast(FP8X4), lhsT_scale=w3_q[m // 2][1][:, m_cols],
+                    rhs=hz_codes[:, cols].bitcast(FP8X4), rhs_scale=hz_bytes[:, cols], start=True, stop=False,
+                )
+                nc.tensor.matmul_mx(
+                    bank[:, cols], lhsT=w2_q[m // 2][0][:, m_cols].bitcast(FP8X4), lhsT_scale=w2_q[m // 2][1][:, m_cols],
+                    rhs=z_q[half][0][:].bitcast(FP8X4), rhs_scale=z_q[half][1][:], start=False, stop=True,
+                )
+            return bank
+
+        w3_grouped1 = interleave("w3_grouped1", w3_raw[1], nc.scalar.copy)
+        w2_grouped1 = interleave("w2_grouped1", w2_raw[1], nc.scalar.copy)
+        nc.scalar.copy(h_rows[0][:, :S], h_products(0)[:])
+        nc.vector.tensor_copy(h_rows[1][:, :S], h_products(1)[:])
+        w3_q.append(quantize_half("w3_1", w3_grouped1))
+        w2_q.append(quantize_half("w2_1", w2_grouped1))
+        late_banks = {m: h_products(m) for m in (2, 3)}
+
+        widths = [(256, 256), (256, 256), (256, 128, 128), (128, 128, 128, 64, 64)]
+        pieces = [(m, sum(widths[m][:i]), widths[m][i]) for m in range(4) for i in range(len(widths[m]))]
+        results = [keep.tile([P, S], F32, name="result%d" % m) for m in range(4)]
+        stored = [0, 0, 0, 0]
+
+        def finish(m, first, width, largest, smallest):
+            end = first + width
+            nc.vector.scalar_tensor_tensor(results[m][:, first:end], smallest[:], -0.5, largest[:], MULT, ADD)
+            if end % HALF == 0 or (m, end) == (3, 384):
+                nc.sync.dma_start(out[m * P : (m + 1) * P, stored[m] : end], results[m][:, stored[m] : end])
+                stored[m] = end
+
+        waiting = None
+        for m, first, width in pieces:
+            tag = "%d_%d" % (m, first)
+            members = keep.tile([P, width, MEMBERS], F32, name="members" + tag)
+            flat = members[:].rearrange("p c i -> p (c i)")
+            count = min(GATHER, width * MEMBERS)
+            for start in range(0, width * MEMBERS, count):
+                by_n3 = entries(n3_t, first * MEMBERS + start, count)
+                nc.scalar.activation(flat[:, start : start + count], h_rows[m][:].indirect(by_n3), COPY)
+            low_pairs = keep.tile([P, width, 2], F32, name="low_pairs" + tag)
+            high_pairs = keep.tile([P, width, 2], F32, name="high_pairs" + tag)
+            nc.vector.tensor_tensor(low_pairs[:], members[:, :, 0:2], members[:, :, 2:4], MIN)
+            nc.vector.tensor_tensor(high_pairs[:], members[:, :, 0:2], members[:, :, 2:4], MAX)
+            if waiting is not None:
+                finish(*waiting)
+            smallest = keep.tile([P, width], F32, name="smallest" + tag)
+            largest = keep.tile([P, width], F32, name="largest" + tag)
+            nc.vector.tensor_tensor(smallest[:], low_pairs[:, :, 0], low_pairs[:, :, 1], MIN)
+            nc.vector.tensor_tensor(largest[:], high_pairs[:, :, 0], high_pairs[:, :, 1], MAX)
+            waiting = (m, first, width, largest, smallest)
+            if first == 0 and m + 2 in late_banks:
+                nc.vector.tensor_copy(h_rows[m + 2][:, :S], late_banks[m + 2][:])
+        finish(*waiting)

@@ -23,9 +23,11 @@ PACK = 4
 PER_COLUMN = 16
 HALF = 256
 MEMBERS = 4
-SPARE = 32
-GATHER = 512
-BOTH_ON_SCALAR = 3
+GATHER = 1024
+WINDOW = GATHER + 32
+W1_SCALAR_SHARE = 20
+CHUNKS = ((0, 256), (256, 128), (384, 128))
+BOTH_ON_SCALAR = (2, 3)
 
 
 def entries(list_tile, first, count):
@@ -46,28 +48,21 @@ def tile_picked_mixhprodgspan_none_p_kernel(
             nc.sync.dma_start(list_tile[:], source)
             return list_tile
 
-        def load_weight_half(name, w, half):
-            raw = keep.tile([P, PACK, HALF], F32, name=name)
-            cols = slice(half * HALF, (half + 1) * HALF)
-            nc.sync.dma_start(raw[:], w.rearrange("(p j) c -> p j c", j=PACK)[:, :, cols])
+        def load_weight_columns(name, w, first, end):
+            raw = keep.tile([P, PACK, end - first], F32, name=name)
+            nc.sync.dma_start(raw[:], w.rearrange("(p j) c -> p j c", j=PACK)[:, :, first:end])
             return raw
 
-        def interleave(name, planes, copy=nc.vector.tensor_copy):
-            grouped = keep.tile([P, HALF, PACK], BF16, name=name, align_bytes=64)
+        def interleave(copy, grouped, planes):
             copy(
-                grouped[:].rearrange("p (c i) j -> p c j i", i=4),
-                planes[:].rearrange("p j (c i) -> p c j i", i=4),
+                grouped.rearrange("p (c i) j -> p c j i", i=4),
+                planes.rearrange("p j (c i) -> p c j i", i=4),
             )
-            return grouped
 
-        def quantize(name, flat, width):
+        def mx_tiles(name, width):
             codes = keep.tile([P, width], U32, name=name + "_codes", align_bytes=64)
             scales = keep.tile([P, width], U8, name=name + "_scales", align_bytes=64)
-            nc.vector.quantize_mx(codes[:].bitcast(FP8X4), scales[:], flat)
             return codes, scales
-
-        def quantize_half(name, grouped):
-            return quantize(name, grouped[:].rearrange("p c j -> p (c j)"), HALF)
 
         byte_table = keep.tile([P, T], U8, name="byte_table", align_bytes=64)
         nc.gpsimd.memset(byte_table[:].bitcast(I32), 0)
@@ -82,18 +77,18 @@ def tile_picked_mixhprodgspan_none_p_kernel(
         hz_t = load_list("hz_t", hz)
         word_table = keep.tile([P, T], I32, name="word_table", align_bytes=64)
         nc.sync.dma_start(word_table[:], x_words[0].rearrange("p n t -> p (n t)").bitcast(I32))
-        w1_raw = [load_weight_half("w1_raw%d" % h, w1, h) for h in range(2)]
+        w1_raw = [load_weight_columns("w1_raw%d" % h, w1, h * HALF, (h + 1) * HALF) for h in range(2)]
+        w3_raw = [load_weight_columns("w3_raw0", w3, 0, HALF)]
+        w2_raw = [load_weight_columns("w2_raw0", w2, 0, HALF)]
         n1_t = load_list("n1_t", n1)
         n2_t = load_list("n2_t", n2)
         gain = keep.tile([P, PACK], F32, name="gain")
         nc.sync.dma_start(gain[:], gn.rearrange("(p t) o -> p (t o)", t=PACK))
-        w3_raw = [load_weight_half("w3_raw0", w3, 0)]
-        w2_raw = [load_weight_half("w2_raw0", w2, 0)]
         n3_t = load_list("n3_t", n3)
-        w3_raw.append(load_weight_half("w3_raw1", w3, 1))
-        w2_raw.append(load_weight_half("w2_raw1", w2, 1))
+        w3_raw.append(load_weight_columns("w3_raw1", w3, HALF, N))
+        w2_raw.append(load_weight_columns("w2_raw1", w2, HALF, N))
 
-        h_rows = [keep.tile([P, S + SPARE], F32, name="h_rows%d" % m) for m in range(4)]
+        h_rows = [keep.tile([P, WINDOW], F32, name="h_rows%d" % m) for m in range(4)]
         for m in range(4):
             nc.gpsimd.memset(h_rows[m][:, S:], 0.0)
 
@@ -106,93 +101,123 @@ def tile_picked_mixhprodgspan_none_p_kernel(
         x_bytes = gather_packed("x_bytes", byte_table[:], U8, offs_t)
         hz_bytes_raw = gather_packed("hz_bytes_raw", byte_table[:], U8, hz_t)
         x_codes = gather_packed("x_codes", words, U32, offs_t)
-
         hz_bytes = keep.tile([P, S], U8, name="hz_bytes", align_bytes=64)
         nc.vector.tensor_copy(hz_bytes[:].bitcast(I32), hz_bytes_raw[:].bitcast(I32))
-
-        w1_grouped = keep.tile([P, PACK, P, PACK], BF16, name="w1_grouped", align_bytes=64)
-        for half in range(2):
-            dst = w1_grouped[:, :, half * 64 : (half + 1) * 64, :].rearrange("p t m j -> p m t j")
-            src = w1_raw[half][:].rearrange("p j (m t) -> p m t j", t=PACK)
-            if half == 0:
-                nc.scalar.copy(dst, src)
-            else:
-                nc.vector.tensor_copy(dst, src)
-        w1_q = [
-            quantize("w1_%d" % t, w1_grouped[:, t, :, :].rearrange("p m j -> p (m j)"), P)
-            for t in range(PACK)
-        ]
         hz_codes = gather_packed("hz_codes", words, U32, hz_t)
         for u in range(2):
             nc.sync.dma_start(
                 hz_bytes[2 + u : P : 32, :].bitcast(I32), hz_bytes_raw[16 + u : P : 32, :].bitcast(I32)
             )
 
+        w1_grouped = keep.tile([P, PACK, P, PACK], BF16, name="w1_grouped", align_bytes=64)
+        shares = (
+            (nc.scalar.copy, 0, 0, 64),
+            (nc.scalar.copy, 1, 0, W1_SCALAR_SHARE),
+            (nc.vector.tensor_copy, 1, W1_SCALAR_SHARE, 64),
+        )
+        for copy, half, lo, hi in shares:
+            dst = w1_grouped[:, :, half * 64 + lo : half * 64 + hi, :].rearrange("p t m j -> p m t j")
+            src = w1_raw[half][:].rearrange("p j (m t) -> p m t j", t=PACK)[:, lo:hi, :, :]
+            copy(dst, src)
+
         y_rows = []
         for t in range(PACK):
+            codes, scales = mx_tiles("w1_%d" % t, P)
+            nc.vector.quantize_mx(
+                codes[:].bitcast(FP8X4), scales[:], w1_grouped[:, t, :, :].rearrange("p m j -> p (m j)")
+            )
             bank = psum.tile([P, S], F32, name="y_bank%d" % t)
-            codes, scales = w1_q[t]
             nc.tensor.matmul_mx(
                 bank[:], lhsT=codes[:].bitcast(FP8X4), lhsT_scale=scales[:],
                 rhs=x_codes[:].bitcast(FP8X4), rhs_scale=x_bytes[:], start=True, stop=True,
             )
             rows = keep.tile([P, S], F32, name="y_rows%d" % t)
-            nc.scalar.copy(rows[:], bank[:])
+            leave_bank = nc.scalar.copy if t % 2 == 0 else nc.vector.tensor_copy
+            leave_bank(rows[:], bank[:])
             y_rows.append(rows)
 
-        w3_q = [quantize_half("w3_0", interleave("w3_grouped0", w3_raw[0]))]
+        def group_weights(m, copies, tag):
+            grouped = keep.tile([P, 2, P, PACK], BF16, name="w_grouped%d" % m, tag=tag, align_bytes=64)
+            cols = slice((m % 2) * P, (m % 2 + 1) * P)
+            for side, raw in enumerate((w3_raw, w2_raw)):
+                interleave(copies[side], grouped[:, side, :, :], raw[m // 2][:, :, cols])
+            return grouped
+
+        def quantize_weights(m, grouped):
+            codes, scales = mx_tiles("w_%d" % m, 2 * P)
+            nc.vector.quantize_mx(codes[:].bitcast(FP8X4), scales[:], grouped[:].rearrange("p s c j -> p (s c j)"))
+            return codes, scales
 
         gained = {}
         for t in range(PACK):
-            if t != BOTH_ON_SCALAR:
+            if t not in BOTH_ON_SCALAR:
                 gained[t] = keep.tile([P, S], F32, name="gained%d" % t)
                 nc.vector.tensor_scalar(gained[t][:], y_rows[t][:], gain[:, t : t + 1], None, MULT)
 
-        def z_planes(half):
-            planes = keep.tile([P, PACK, HALF], F32, name="z_planes%d" % half)
-            by_n1 = entries(n1_t, half * HALF, HALF)
-            by_n2 = entries(n2_t, half * HALF, HALF)
+        z_codes, z_scales = mx_tiles("z", S)
+
+        ring = []
+
+        def gather_on_scalar(rows, offsets, width):
+            ring.append(keep.tile([P, width], F32, name="picked%d" % len(ring), align_bytes=64))
+            nc.scalar.activation(ring[-1][:], rows[:].indirect(offsets), COPY)
+            return ring[-1]
+
+        def make_z(first, width, tag):
+            planes = keep.tile([P, PACK, width], F32, name="z_planes%d" % first)
+            by_n1 = entries(n1_t, first, width)
+            by_n2 = entries(n2_t, first, width)
             for t in range(PACK):
-                first = keep.tile([P, HALF], F32, name="first%d_%d" % (half, t))
-                nc.scalar.activation(first[:], y_rows[t][:].indirect(by_n1), COPY)
-                if t == BOTH_ON_SCALAR:
-                    second = keep.tile([P, HALF], F32, name="second%d" % half)
-                    nc.scalar.activation(second[:], y_rows[t][:].indirect(by_n2), COPY)
+                at_n1 = gather_on_scalar(y_rows[t], by_n1, width)
+                if t in BOTH_ON_SCALAR:
+                    at_n2 = gather_on_scalar(y_rows[t], by_n2, width)
                     nc.vector.scalar_tensor_tensor(
-                        planes[:, t, :], first[:], gain[:, t : t + 1], second[:], MULT, MULT
+                        planes[:, t, :], at_n1[:], gain[:, t : t + 1], at_n2[:], MULT, MULT
                     )
                 else:
-                    nc.vector.tensor_tensor(planes[:, t, :], gained[t][:].indirect(by_n2), first[:], MULT)
-            return planes
+                    nc.vector.tensor_tensor(planes[:, t, :], gained[t][:].indirect(by_n2), at_n1[:], MULT)
+            grouped = keep.tile([P, width, PACK], BF16, name="z_grouped%d" % first, tag=tag, align_bytes=64)
+            interleave(nc.vector.tensor_copy, grouped[:], planes[:])
+            cols = slice(first, first + width)
+            nc.vector.quantize_mx(
+                z_codes[:, cols].bitcast(FP8X4), z_scales[:, cols], grouped[:].rearrange("p c j -> p (c j)")
+            )
 
-        z_grouped0 = interleave("z_grouped0", z_planes(0))
-        w2_grouped0 = interleave("w2_grouped0", w2_raw[0])
-        z_q = [quantize_half("z_0", z_grouped0)]
-        w2_q = [quantize_half("w2_0", w2_grouped0)]
-        z_q.append(quantize_half("z_1", interleave("z_grouped1", z_planes(1))))
+        def h_product(target, weights, cols):
+            codes, scales = weights
+            moving = ((hz_codes, hz_bytes), (z_codes, z_scales))
+            for side in range(2):
+                m_cols = slice(side * P, (side + 1) * P)
+                nc.tensor.matmul_mx(
+                    target, lhsT=codes[:, m_cols].bitcast(FP8X4), lhsT_scale=scales[:, m_cols],
+                    rhs=moving[side][0][:, cols].bitcast(FP8X4), rhs_scale=moving[side][1][:, cols],
+                    start=(side == 0), stop=(side == 1),
+                )
 
-        def h_products(m):
+        weights0 = quantize_weights(0, group_weights(0, (nc.scalar.copy, nc.vector.tensor_copy), "w_grouped0"))
+        grouped1 = group_weights(1, (nc.vector.tensor_copy, nc.vector.tensor_copy), "w_grouped1")
+        early_bank = psum.tile([P, S], F32, name="h_bank0")
+        for first, width in CHUNKS[:-1]:
+            make_z(first, width, "z_grouped%d" % first)
+            h_product(early_bank[:, first : first + width], weights0, slice(first, first + width))
+        last_first, last_width = CHUNKS[-1]
+        make_z(last_first, last_width, "staging")
+        nc.scalar.copy(h_rows[0][:, :last_first], early_bank[:, :last_first])
+        grouped2 = group_weights(2, (nc.scalar.copy, nc.scalar.copy), "picked%d" % (len(ring) - 3))
+        last_bank = psum.tile([P, last_width], F32, name="h_last", tag="y_bank0")
+        h_product(last_bank[:], weights0, slice(last_first, S))
+        nc.scalar.copy(h_rows[0][:, last_first:S], last_bank[:])
+
+        for m in (1, 2, 3):
+            if m < 3:
+                grouped = (grouped1, grouped2)[m - 1]
+            else:
+                grouped = group_weights(m, (nc.vector.tensor_copy, nc.vector.tensor_copy), "staging")
+            weights = quantize_weights(m, grouped)
             bank = psum.tile([P, S], F32, name="h_bank%d" % m)
-            m_cols = slice((m % 2) * P, (m % 2 + 1) * P)
-            for half in range(2):
-                cols = slice(half * HALF, (half + 1) * HALF)
-                nc.tensor.matmul_mx(
-                    bank[:, cols], lhsT=w3_q[m // 2][0][:, m_cols].bitcast(FP8X4), lhsT_scale=w3_q[m // 2][1][:, m_cols],
-                    rhs=hz_codes[:, cols].bitcast(FP8X4), rhs_scale=hz_bytes[:, cols], start=True, stop=False,
-                )
-                nc.tensor.matmul_mx(
-                    bank[:, cols], lhsT=w2_q[m // 2][0][:, m_cols].bitcast(FP8X4), lhsT_scale=w2_q[m // 2][1][:, m_cols],
-                    rhs=z_q[half][0][:].bitcast(FP8X4), rhs_scale=z_q[half][1][:], start=False, stop=True,
-                )
-            return bank
-
-        w3_grouped1 = interleave("w3_grouped1", w3_raw[1], nc.scalar.copy)
-        w2_grouped1 = interleave("w2_grouped1", w2_raw[1], nc.scalar.copy)
-        nc.scalar.copy(h_rows[0][:, :S], h_products(0)[:])
-        nc.vector.tensor_copy(h_rows[1][:, :S], h_products(1)[:])
-        w3_q.append(quantize_half("w3_1", w3_grouped1))
-        w2_q.append(quantize_half("w2_1", w2_grouped1))
-        late_banks = {m: h_products(m) for m in (2, 3)}
+            h_product(bank[:], weights, slice(0, S))
+            leave_bank = nc.scalar.copy if m == 1 else nc.vector.tensor_copy
+            leave_bank(h_rows[m][:, :S], bank[:])
 
         widths = [(256, 256), (256, 256), (256, 128, 128), (128, 128, 128, 64, 64)]
         pieces = [(m, sum(widths[m][:i]), widths[m][i]) for m in range(4) for i in range(len(widths[m]))]
@@ -207,18 +232,20 @@ def tile_picked_mixhprodgspan_none_p_kernel(
                 stored[m] = end
 
         waiting = None
+        free_tag = "staging"
         for m, first, width in pieces:
             tag = "%d_%d" % (m, first)
-            members = keep.tile([P, width, MEMBERS], F32, name="members" + tag)
+            members = keep.tile([P, width, MEMBERS], F32, name="members" + tag, align_bytes=64)
             flat = members[:].rearrange("p c i -> p (c i)")
             count = min(GATHER, width * MEMBERS)
             for start in range(0, width * MEMBERS, count):
                 by_n3 = entries(n3_t, first * MEMBERS + start, count)
                 nc.scalar.activation(flat[:, start : start + count], h_rows[m][:].indirect(by_n3), COPY)
-            low_pairs = keep.tile([P, width, 2], F32, name="low_pairs" + tag)
-            high_pairs = keep.tile([P, width, 2], F32, name="high_pairs" + tag)
-            nc.vector.tensor_tensor(low_pairs[:], members[:, :, 0:2], members[:, :, 2:4], MIN)
-            nc.vector.tensor_tensor(high_pairs[:], members[:, :, 0:2], members[:, :, 2:4], MAX)
+            pairs = keep.tile([P, 2, width, 2], F32, name="pairs" + tag, tag=free_tag, align_bytes=64)
+            free_tag = "members" + tag
+            low_pairs, high_pairs = pairs[:, 0, :, :], pairs[:, 1, :, :]
+            nc.vector.tensor_tensor(low_pairs, members[:, :, 0:2], members[:, :, 2:4], MIN)
+            nc.vector.tensor_tensor(high_pairs, members[:, :, 0:2], members[:, :, 2:4], MAX)
             if waiting is not None:
                 finish(*waiting)
             smallest = keep.tile([P, width], F32, name="smallest" + tag)
@@ -226,6 +253,4 @@ def tile_picked_mixhprodgspan_none_p_kernel(
             nc.vector.tensor_tensor(smallest[:], low_pairs[:, :, 0], low_pairs[:, :, 1], MIN)
             nc.vector.tensor_tensor(largest[:], high_pairs[:, :, 0], high_pairs[:, :, 1], MAX)
             waiting = (m, first, width, largest, smallest)
-            if first == 0 and m + 2 in late_banks:
-                nc.vector.tensor_copy(h_rows[m + 2][:, :S], late_banks[m + 2][:])
         finish(*waiting)

from contextlib import ExitStack

import concourse.mybir as mybir

K, T, S, N, H, W = 512, 2048, 512, 512, 512, 2048
FLOPS = 3 * 2 * 512 * 512 * 512

F32 = mybir.dt.float32
BF16 = mybir.dt.bfloat16
I32 = mybir.dt.int32
U32 = mybir.dt.uint32
U16 = mybir.dt.uint16
U8 = mybir.dt.uint8
FP8X4 = mybir.dt.float8_e4m3fn_x4
COPY = mybir.ActivationFunctionType.Copy
MULT = mybir.AluOpType.mult
ADD = mybir.AluOpType.add
MAX = mybir.AluOpType.max
MIN = mybir.AluOpType.min

P = 128
PACK = 4
PER_COLUMN = 16
HALF = 256
MEMBERS = 4
GATHER = 1024
WINDOW = GATHER + 32
W1_SCALAR_SHARE = 20
CHUNKS = ((0, 256), (256, 128), (384, 128))
BOTH_ON_SCALAR = (2, 3)


def entries(list_tile, first, count):
    return list_tile[:, first // PER_COLUMN : (first + count) // PER_COLUMN]


def tile_picked_mixhprodgspan_none_p_kernel(
    tc, x_words, x_scales, w1, gn, w2, w3, offs, n1, n2, hz, n3, out
):
    nc = tc.nc
    with ExitStack() as ctx:
        lists = ctx.enter_context(tc.tile_pool(name="lists", bufs=1))
        keep = ctx.enter_context(tc.tile_pool(name="keep", bufs=1))
        psum = ctx.enter_context(tc.psum_pool(name="psum", bufs=1))

        def load_list(name, source):
            list_tile = lists.tile([P, source.shape[1]], U16, name=name)
            nc.sync.dma_start(list_tile[:], source)
            return list_tile

        def load_weight_columns(name, w, first, end):
            raw = keep.tile([P, PACK, end - first], F32, name=name)
            nc.sync.dma_start(raw[:], w.rearrange("(p j) c -> p j c", j=PACK)[:, :, first:end])
            return raw

        def interleave(copy, grouped, planes):
            copy(
                grouped.rearrange("p (c i) j -> p c j i", i=4),
                planes.rearrange("p j (c i) -> p c j i", i=4),
            )

        def mx_tiles(name, width):
            codes = keep.tile([P, width], U32, name=name + "_codes", align_bytes=64)
            scales = keep.tile([P, width], U8, name=name + "_scales", align_bytes=64)
            return codes, scales

        byte_table = keep.tile([P, T], U8, name="byte_table", align_bytes=64)
        nc.gpsimd.memset(byte_table[:].bitcast(I32), 0)
        scale_rows = x_scales[0]
        for u in range(4):
            partition_step, row_step = (16, 2) if u < 2 else (32, 4)
            nc.sync.dma_start(
                byte_table[u:P:partition_step, :].bitcast(I32),
                scale_rows[u:16:row_step, :].bitcast(I32),
            )
        offs_t = load_list("offs_t", offs)
        hz_t = load_list("hz_t", hz)
        word_table = keep.tile([P, T], I32, name="word_table", align_bytes=64)
        nc.sync.dma_start(word_table[:], x_words[0].rearrange("p n t -> p (n t)").bitcast(I32))
        w1_raw = [load_weight_columns("w1_raw%d" % h, w1, h * HALF, (h + 1) * HALF) for h in range(2)]
        w3_raw = [load_weight_columns("w3_raw0", w3, 0, HALF)]
        w2_raw = [load_weight_columns("w2_raw0", w2, 0, HALF)]
        n1_t = load_list("n1_t", n1)
        n2_t = load_list("n2_t", n2)
        gain = keep.tile([P, PACK], F32, name="gain")
        nc.sync.dma_start(gain[:], gn.rearrange("(p t) o -> p (t o)", t=PACK))
        n3_t = load_list("n3_t", n3)
        w3_raw.append(load_weight_columns("w3_raw1", w3, HALF, N))
        w2_raw.append(load_weight_columns("w2_raw1", w2, HALF, N))

        h_rows = [keep.tile([P, WINDOW], F32, name="h_rows%d" % m) for m in range(4)]
        for m in range(4):
            nc.gpsimd.memset(h_rows[m][:, S:], 0.0)

        def gather_packed(name, table, dtype, list_tile):
            picked = keep.tile([P, S], dtype, name=name, align_bytes=64)
            nc.vector.tensor_copy(picked[:], table.indirect(list_tile[:]))
            return picked

        words = word_table[:].bitcast(U32)
        x_bytes = gather_packed("x_bytes", byte_table[:], U8, offs_t)
        hz_bytes_raw = gather_packed("hz_bytes_raw", byte_table[:], U8, hz_t)
        x_codes = gather_packed("x_codes", words, U32, offs_t)
        hz_bytes = keep.tile([P, S], U8, name="hz_bytes", align_bytes=64)
        nc.vector.tensor_copy(hz_bytes[:].bitcast(I32), hz_bytes_raw[:].bitcast(I32))
        hz_codes = gather_packed("hz_codes", words, U32, hz_t)
        for u in range(2):
            nc.sync.dma_start(
                hz_bytes[2 + u : P : 32, :].bitcast(I32), hz_bytes_raw[16 + u : P : 32, :].bitcast(I32)
            )

        w1_grouped = keep.tile([P, PACK, P, PACK], BF16, name="w1_grouped", align_bytes=64)
        shares = (
            (nc.scalar.copy, 0, 0, 64),
            (nc.scalar.copy, 1, 0, W1_SCALAR_SHARE),
            (nc.vector.tensor_copy, 1, W1_SCALAR_SHARE, 64),
        )
        for copy, half, lo, hi in shares:
            dst = w1_grouped[:, :, half * 64 + lo : half * 64 + hi, :].rearrange("p t m j -> p m t j")
            src = w1_raw[half][:].rearrange("p j (m t) -> p m t j", t=PACK)[:, lo:hi, :, :]
            copy(dst, src)

        y_rows = []
        for t in range(PACK):
            codes, scales = mx_tiles("w1_%d" % t, P)
            nc.vector.quantize_mx(
                codes[:].bitcast(FP8X4), scales[:], w1_grouped[:, t, :, :].rearrange("p m j -> p (m j)")
            )
            bank = psum.tile([P, S], F32, name="y_bank%d" % t)
            nc.tensor.matmul_mx(
                bank[:], lhsT=codes[:].bitcast(FP8X4), lhsT_scale=scales[:],
                rhs=x_codes[:].bitcast(FP8X4), rhs_scale=x_bytes[:], start=True, stop=True,
            )
            rows = keep.tile([P, S], F32, name="y_rows%d" % t)
            leave_bank = nc.scalar.copy if t % 2 == 0 else nc.vector.tensor_copy
            leave_bank(rows[:], bank[:])
            y_rows.append(rows)

        def group_weights(m, copies, tag):
            grouped = keep.tile([P, 2, P, PACK], BF16, name="w_grouped%d" % m, tag=tag, align_bytes=64)
            cols = slice((m % 2) * P, (m % 2 + 1) * P)
            for side, raw in enumerate((w3_raw, w2_raw)):
                interleave(copies[side], grouped[:, side, :, :], raw[m // 2][:, :, cols])
            return grouped

        def quantize_weights(m, grouped):
            codes, scales = mx_tiles("w_%d" % m, 2 * P)
            nc.vector.quantize_mx(codes[:].bitcast(FP8X4), scales[:], grouped[:].rearrange("p s c j -> p (s c j)"))
            return codes, scales

        gained = {}
        for t in range(PACK):
            if t not in BOTH_ON_SCALAR:
                gained[t] = keep.tile([P, S], F32, name="gained%d" % t)
                nc.vector.tensor_scalar(gained[t][:], y_rows[t][:], gain[:, t : t + 1], None, MULT)

        z_codes, z_scales = mx_tiles("z", S)

        ring = []

        def gather_on_scalar(rows, offsets, width):
            ring.append(keep.tile([P, width], F32, name="picked%d" % len(ring), align_bytes=64))
            nc.scalar.activation(ring[-1][:], rows[:].indirect(offsets), COPY)
            return ring[-1]

        def make_z(first, width, tag):
            planes = keep.tile([P, PACK, width], F32, name="z_planes%d" % first)
            by_n1 = entries(n1_t, first, width)
            by_n2 = entries(n2_t, first, width)
            for t in range(PACK):
                at_n1 = gather_on_scalar(y_rows[t], by_n1, width)
                if t in BOTH_ON_SCALAR:
                    at_n2 = gather_on_scalar(y_rows[t], by_n2, width)
                    nc.vector.scalar_tensor_tensor(
                        planes[:, t, :], at_n1[:], gain[:, t : t + 1], at_n2[:], MULT, MULT
                    )
                else:
                    nc.vector.tensor_tensor(planes[:, t, :], gained[t][:].indirect(by_n2), at_n1[:], MULT)
            grouped = keep.tile([P, width, PACK], BF16, name="z_grouped%d" % first, tag=tag, align_bytes=64)
            interleave(nc.vector.tensor_copy, grouped[:], planes[:])
            cols = slice(first, first + width)
            nc.vector.quantize_mx(
                z_codes[:, cols].bitcast(FP8X4), z_scales[:, cols], grouped[:].rearrange("p c j -> p (c j)")
            )

        def h_product(target, weights, cols):
            codes, scales = weights
            moving = ((hz_codes, hz_bytes), (z_codes, z_scales))
            for side in range(2):
                m_cols = slice(side * P, (side + 1) * P)
                nc.tensor.matmul_mx(
                    target, lhsT=codes[:, m_cols].bitcast(FP8X4), lhsT_scale=scales[:, m_cols],
                    rhs=moving[side][0][:, cols].bitcast(FP8X4), rhs_scale=moving[side][1][:, cols],
                    start=(side == 0), stop=(side == 1),
                )

        weights0 = quantize_weights(0, group_weights(0, (nc.scalar.copy, nc.vector.tensor_copy), "w_grouped0"))
        grouped1 = group_weights(1, (nc.vector.tensor_copy, nc.vector.tensor_copy), "w_grouped1")
        early_bank = psum.tile([P, S], F32, name="h_bank0")
        for first, width in CHUNKS[:-1]:
            make_z(first, width, "z_grouped%d" % first)
            h_product(early_bank[:, first : first + width], weights0, slice(first, first + width))
        last_first, last_width = CHUNKS[-1]
        make_z(last_first, last_width, "staging")
        nc.scalar.copy(h_rows[0][:, :last_first], early_bank[:, :last_first])
        grouped2 = group_weights(2, (nc.scalar.copy, nc.scalar.copy), "picked%d" % (len(ring) - 3))
        last_bank = psum.tile([P, last_width], F32, name="h_last", tag="y_bank0")
        h_product(last_bank[:], weights0, slice(last_first, S))
        nc.scalar.copy(h_rows[0][:, last_first:S], last_bank[:])

        for m in (1, 2, 3):
            if m < 3:
                grouped = (grouped1, grouped2)[m - 1]
            else:
                grouped = group_weights(m, (nc.vector.tensor_copy, nc.vector.tensor_copy), "staging")
            weights = quantize_weights(m, grouped)
            bank = psum.tile([P, S], F32, name="h_bank%d" % m)
            h_product(bank[:], weights, slice(0, S))
            leave_bank = nc.scalar.copy if m == 1 else nc.vector.tensor_copy
            leave_bank(h_rows[m][:, :S], bank[:])

        widths = [(256, 256), (256, 256), (256, 128, 128), (128, 128, 128, 64, 64)]
        pieces = [(m, sum(widths[m][:i]), widths[m][i]) for m in range(4) for i in range(len(widths[m]))]
        results = [keep.tile([P, S], F32, name="result%d" % m) for m in range(4)]
        stored = [0, 0, 0, 0]

        def finish(m, first, width, largest, smallest):
            end = first + width
            nc.vector.scalar_tensor_tensor(results[m][:, first:end], smallest[:], -0.5, largest[:], MULT, ADD)
            if end % HALF == 0 or (m, end) == (3, 384):
                nc.sync.dma_start(out[m * P : (m + 1) * P, stored[m] : end], results[m][:, stored[m] : end])
                stored[m] = end

        waiting = None
        free_tag = "staging"
        for m, first, width in pieces:
            tag = "%d_%d" % (m, first)
            members = keep.tile([P, width, MEMBERS], F32, name="members" + tag, align_bytes=64)
            flat = members[:].rearrange("p c i -> p (c i)")
            count = min(GATHER, width * MEMBERS)
            for start in range(0, width * MEMBERS, count):
                by_n3 = entries(n3_t, first * MEMBERS + start, count)
                nc.scalar.activation(flat[:, start : start + count], h_rows[m][:].indirect(by_n3), COPY)
            pairs = keep.tile([P, 2, width, 2], F32, name="pairs" + tag, tag=free_tag, align_bytes=64)
            free_tag = "members" + tag
            low_pairs, high_pairs = pairs[:, 0, :, :], pairs[:, 1, :, :]
            nc.vector.tensor_tensor(low_pairs, members[:, :, 0:2], members[:, :, 2:4], MIN)
            nc.vector.tensor_tensor(high_pairs, members[:, :, 0:2], members[:, :, 2:4], MAX)
            if waiting is not None:
                finish(*waiting)
            smallest = keep.tile([P, width], F32, name="smallest" + tag)
            largest = keep.tile([P, width], F32, name="largest" + tag)
            nc.vector.tensor_tensor(smallest[:], low_pairs[:, :, 0], low_pairs[:, :, 1], MIN)
            nc.vector.tensor_tensor(largest[:], high_pairs[:, :, 0], high_pairs[:, :, 1], MAX)
            waiting = (m, first, width, largest, smallest)
        finish(*waiting)
